import numpy as np
import ml_dtypes


def mxq(x, axis, fmt="e4m3"):
    dtype, down = {"e4m3": (ml_dtypes.float8_e4m3fn, 7), "e5m2": (ml_dtypes.float8_e5m2, 14)}[fmt]
    v = np.moveaxis(np.asarray(x, np.float32).astype(ml_dtypes.bfloat16).astype(np.float64), axis, -1)
    blocks = v.reshape(v.shape[:-1] + (-1, 32))
    amax = np.abs(blocks).max(-1, keepdims=True)
    byte = np.maximum(np.where(amax > 0, np.frexp(amax)[1] - 1 + 127, 0) - down, 1)
    scale = np.exp2(byte - 127.0)
    codes = (blocks / scale).astype(np.float32).astype(dtype).astype(np.float64)
    return np.moveaxis((codes * scale).reshape(v.shape), -1, axis)


WIDE = False


def mx_kscale(k):
    if not WIDE:
        return np.ones(k)
    levels = np.array([10, -10, 5, -5, 0])
    if k % 512:
        return np.exp2(np.random.permutation(np.resize(levels, k // 32))).repeat(32)
    a = np.empty((k // 512, 16))
    for p in range(k // 512):
        a[p, :8] = np.random.permutation(np.resize(levels, 8))
        for g in range(8):
            far = levels[np.abs(levels - a[p, g]) >= 10]
            a[p, g + 8] = far[np.random.randint(len(far))]
    return np.exp2(a.ravel()).repeat(32)


def f64(x):
    return np.asarray(x).astype(np.float64)


def striped(idx):
    return np.tile(idx.reshape(-1, 16).T, (8, 1)).astype(np.uint16)


def unstriped(offs):
    return offs[:16].T.reshape(-1).astype(np.int64)


def relu(v):
    return np.maximum(v, 0.0)


K, T, D, S, V, H, N = 1024, 2048, 4, 512, 256, 1024, 512
P = 2 ** 7


def setup_inputs():
    n = np.random.standard_normal
    s = mx_kscale(K)[:, None]
    u = mx_kscale(H)
    q = np.random.permutation(S)
    return {
        "xT": (n((K, T)) * s).astype(np.float32),
        "w1": (n((K, H)) / np.sqrt(K) / s * u).astype(np.float32),
        "w2": (n((H, N)) / np.sqrt(H) / u[:, None]).astype(np.float32),
        "gate": np.tile(np.random.uniform(0.2, 1.0, (D, 1, V)) / np.sqrt(D), (1, P, 1)).astype(np.float32),
        "offs": striped(np.random.permutation(T)[:S]),
        "pos1": striped(q[:V]),
        "pos2": striped(q[V:]),
        "pos3": striped(np.random.permutation(S)[:V]),
        "pos4": striped(np.random.permutation(S)[:V]),
    }


def reference(xT, w1, w2, gate, offs, pos1, pos2, pos3, pos4):
    h = relu(mxq(f64(w1), 0, "e4m3").T @ mxq(f64(xT)[:, unstriped(offs)], 0, "e4m3"))
    z = sum(f64(gate)[d, :1] * h[:, unstriped(p)] for d, p in enumerate((pos1, pos2, pos3, pos4)))
    return mxq(f64(w2), 0, "e4m3").T @ mxq(z, 0, "e4m3")

@@ -1,0 +1,271 @@
+from contextlib import ExitStack
+
+import concourse.mybir as mybir
+from concourse.masks import make_identity
+
+K, T, D, S, V, H, N = 1024, 2048, 4, 512, 256, 1024, 512
+P = 128
+PACK = 4
+K_PASS = P * PACK
+PASSES = K // K_PASS
+BLOCKS = H // P
+FLOPS = 2 * S * K * H + 2 * V * H * N + 2 * D * V * H
+
+F32 = mybir.dt.float32
+BF16 = mybir.dt.bfloat16
+U32 = mybir.dt.uint32
+U16 = mybir.dt.uint16
+U8 = mybir.dt.uint8
+FP8X4 = mybir.dt.float8_e4m3fn_x4
+RELU = mybir.ActivationFunctionType.Relu
+MULT = mybir.AluOpType.mult
+
+W1_CHUNKS = (128, 128, 256, 512)
+
+
+def tile_picked_sage_relu_e_kernel(
+    tc, xT, w1, w2, gate, offs, pos1, pos2, pos3, pos4, out
+):
+    nc = tc.nc
+    with ExitStack() as ctx:
+        lists = ctx.enter_context(tc.tile_pool(name="lists", bufs=1))
+        keep = ctx.enter_context(tc.tile_pool(name="keep", bufs=1))
+        hpool = ctx.enter_context(tc.tile_pool(name="hpool", bufs=4))
+        prods = ctx.enter_context(tc.tile_pool(name="prods", bufs=12))
+        psum = ctx.enter_context(tc.psum_pool(name="psum", bufs=4))
+
+        offs_sb = lists.tile([P, S // 16], U16, name="offs_sb")
+        pos_sb = [lists.tile([P, V // 16], U16, name=f"pos_sb{d}") for d in range(D)]
+
+        ident = keep.tile([P, P], F32, name="ident")
+        make_identity(nc, ident[:])
+        warm = keep.tile([P, 1], F32, name="warm")
+        nc.gpsimd.memset(warm[:], 0.0)
+        warm_out = keep.tile([P, 1], F32, name="warm_out")
+        nc.scalar.activation(warm_out[:], warm[:], RELU)
+
+        x_raw = [[keep.tile([P, T], F32, name=f"x_raw{s}_{j}") for j in range(PACK)] for s in range(PASSES)]
+        w1_raw = [keep.tile([P, PASSES, PACK, w], F32, name=f"w1_raw{c}") for c, w in enumerate(W1_CHUNKS)]
+        w2_raw = [keep.tile([P, PACK, N], F32, name=f"w2_raw{s}") for s in range(PASSES)]
+        gate_sb = keep.tile([P, D, V], F32, name="gate_sb")
+
+        def load_x(s, j):
+            rows = xT[s * K_PASS : (s + 1) * K_PASS, :].rearrange("(p j) t -> j p t", j=PACK)
+            nc.sync.dma_start(out=x_raw[s][j][:], in_=rows[j])
+
+        def load_w1(c, s_range=range(PASSES)):
+            first = sum(W1_CHUNKS[:c])
+            for s in s_range:
+                block = w1[s * K_PASS : (s + 1) * K_PASS, first : first + W1_CHUNKS[c]]
+                nc.sync.dma_start(out=w1_raw[c][:, s], in_=block.rearrange("(p j) m -> p j m", j=PACK))
+
+        nc.sync.dma_start(offs_sb[:], offs)
+        for s in range(PASSES):
+            for j in range(PACK):
+                if (s, j) == (PASSES - 1, PACK - 1):
+                    load_w1(0, (0,))
+                load_x(s, j)
+                if (s, j) == (0, 0):
+                    for d, pos in enumerate((pos1, pos2, pos3, pos4)):
+                        nc.sync.dma_start(pos_sb[d][:], pos)
+        load_w1(0, (1,))
+        nc.sync.dma_start(out=gate_sb[:], in_=gate.rearrange("d p v -> p d v"))
+        for c in range(1, len(W1_CHUNKS)):
+            load_w1(c)
+        for s in range(PASSES):
+            nc.sync.dma_start(
+                out=w2_raw[s][:], in_=w2[s * K_PASS : (s + 1) * K_PASS, :].rearrange("(p j) n -> p j n", j=PACK)
+            )
+
+        w1_grp = [keep.tile([P, PASSES, w, PACK], BF16, name=f"w1_grp{c}", align_bytes=64) for c, w in enumerate(W1_CHUNKS)]
+        w1_codes = [keep.tile([P, PASSES, w], U32, name=f"w1_codes{c}", align_bytes=64) for c, w in enumerate(W1_CHUNKS)]
+        w1_scales = [keep.tile([P, PASSES, w], U8, name=f"w1_scales{c}", align_bytes=64) for c, w in enumerate(W1_CHUNKS)]
+        w2_grp = [keep.tile([P, N, PACK], BF16, name=f"w2_grp{s}", align_bytes=64) for s in range(PASSES)]
+        w2_codes = [keep.tile([P, N], U32, name=f"w2_codes{s}", align_bytes=64) for s in range(PASSES)]
+        w2_scales = [keep.tile([P, N], U8, name=f"w2_scales{s}", align_bytes=64) for s in range(PASSES)]
+
+        def group_w1(c, s, m0, m1):
+            nc.scalar.copy(
+                out=w1_grp[c][:, s, m0:m1, :], in_=w1_raw[c][:, s, :, m0:m1].rearrange("p j m -> p m j")
+            )
+
+        def quantize_w1(c):
+            nc.vector.quantize_mx(
+                out=w1_codes[c][:].rearrange("p s m -> p (s m)").bitcast(FP8X4),
+                scales=w1_scales[c][:].rearrange("p s m -> p (s m)"),
+                in_=w1_grp[c][:].rearrange("p s m j -> p (s m j)"),
+            )
+
+        def quantize_w1_pass(c, s):
+            nc.vector.quantize_mx(
+                out=w1_codes[c][:, s].bitcast(FP8X4),
+                scales=w1_scales[c][:, s],
+                in_=w1_grp[c][:, s].rearrange("p m j -> p (m j)"),
+            )
+
+        def group_w2(s, n0, n1):
+            nc.scalar.copy(out=w2_grp[s][:, n0:n1, :], in_=w2_raw[s][:, :, n0:n1].rearrange("p j n -> p n j"))
+
+        def quantize_w2(s):
+            nc.vector.quantize_mx(
+                out=w2_codes[s][:].bitcast(FP8X4),
+                scales=w2_scales[s][:],
+                in_=w2_grp[s][:].rearrange("p n j -> p (n j)"),
+            )
+
+        x_grp = [keep.tile([P, S, PACK], BF16, name=f"x_grp{s}", align_bytes=64) for s in range(PASSES)]
+        x_codes = [keep.tile([P, S], U32, name=f"x_codes{s}", align_bytes=64) for s in range(PASSES)]
+        x_scales = [keep.tile([P, S], U8, name=f"x_scales{s}", align_bytes=64) for s in range(PASSES)]
+        HALF = S // 2
+        for s in range(PASSES):
+            last = s == PASSES - 1
+            for j in range(PACK):
+                if last and j == PACK - 1:
+                    for u in range(PASSES):
+                        group_w1(0, u, 0, W1_CHUNKS[0])
+                        if u == 0:
+                            quantize_w1_pass(0, u)
+                    for t in (0, 1):
+                        nc.vector.tensor_copy(
+                            x_grp[s][:, t * HALF : (t + 1) * HALF, j],
+                            x_raw[s][j][:].indirect(offs_sb[:, t * HALF // 16 : (t + 1) * HALF // 16]),
+                        )
+                    quantize_w1_pass(0, 1)
+                else:
+                    nc.vector.tensor_copy(x_grp[s][:, :, j], x_raw[s][j][:].indirect(offs_sb[:]))
+            for t in (0, 1) if last else (None,):
+                cols = slice(0, S) if t is None else slice(t * HALF, (t + 1) * HALF)
+                nc.vector.quantize_mx(
+                    out=x_codes[s][:, cols].bitcast(FP8X4),
+                    scales=x_scales[s][:, cols],
+                    in_=x_grp[s][:, cols, :].rearrange("p t j -> p (t j)"),
+                )
+
+        starts = [sum(W1_CHUNKS[:c]) for c in range(len(W1_CHUNKS))]
+
+        def project(b):
+            c = max(i for i in range(len(W1_CHUNKS)) if starts[i] <= b * P)
+            cols = slice(b * P - starts[c], b * P - starts[c] + P)
+            h = hpool.tile([P, S], F32, name="h")
+            width = HALF if b == 0 else S
+            for t in range(S // width):
+                acc = psum.tile([P, S], F32, name="acc", tag="bank")
+                nodes = slice(t * width, (t + 1) * width)
+                for s in range(PASSES):
+                    nc.tensor.matmul_mx(
+                        out=acc[:, :width],
+                        lhsT=w1_codes[c][:, s, cols].bitcast(FP8X4),
+                        lhsT_scale=w1_scales[c][:, s, cols],
+                        rhs=x_codes[s][:, nodes].bitcast(FP8X4),
+                        rhs_scale=x_scales[s][:, nodes],
+                        start=(s == 0),
+                        stop=(s == PASSES - 1),
+                    )
+                if t == 0:
+                    nc.scalar.activation(h[:, nodes], acc[:, :width], RELU)
+                else:
+                    nc.vector.tensor_relu(h[:, nodes], acc[:, :width])
+            return h
+
+        HALVES = V // P
+        z_t = [keep.tile([P, H], BF16, name=f"z_t{v}", align_bytes=64) for v in range(HALVES)]
+        z_grp = [keep.tile([P, V * PACK], BF16, name=f"z_grp{s}", align_bytes=64) for s in range(PASSES)]
+        z_codes = [keep.tile([P, V], U32, name=f"z_codes{s}", align_bytes=64) for s in range(PASSES)]
+        z_scales = [keep.tile([P, V], U8, name=f"z_scales{s}", align_bytes=64) for s in range(PASSES)]
+        out_acc = {}
+
+        def gather_block(b, h):
+            for d in range(D):
+                prod = prods.tile([P, V], F32, name="prod")
+                nc.vector.tensor_tensor(prod[:], h[:].indirect(pos_sb[d][:]), gate_sb[:, d, :], MULT)
+                for v in range(HALVES):
+                    nc.tensor.matmul(
+                        z_ps[v][:, (b % PACK) * P : (b % PACK + 1) * P],
+                        prod[:, v * P : (v + 1) * P],
+                        ident[:],
+                        start=(d == 0),
+                        stop=(d == D - 1),
+                        is_transpose=True,
+                    )
+
+        def z_out(s, v, b0, b1):
+            eng = nc.vector.tensor_copy if (b1 == PACK and s == PASSES - 1 and v == 1) else nc.scalar.copy
+            eng(out=z_t[v][:, s * K_PASS + b0 * P : s * K_PASS + b1 * P], in_=z_ps[v][:, b0 * P : b1 * P])
+
+        def z_finish(s):
+            words = psum.tile([P, HALVES, 2, P], F32, name="words", tag="words", bufs=2)
+            for v in range(HALVES):
+                zw = z_t[v][:].bitcast(F32)
+                for u in range(2):
+                    nc.tensor.transpose(
+                        words[:, v, u, :], zw[:, s * (K_PASS // 2) + u : (s + 1) * (K_PASS // 2) : 2], ident[:]
+                    )
+            for v, copy in enumerate((nc.scalar.copy, nc.vector.tensor_copy)):
+                copy(
+                    out=z_grp[s][:, v * P * PACK : (v + 1) * P * PACK].bitcast(F32).rearrange("p (n u) -> p n u", u=2),
+                    in_=words[:, v].rearrange("p u n -> p n u"),
+                )
+            nc.vector.quantize_mx(out=z_codes[s][:].bitcast(FP8X4), scales=z_scales[s][:], in_=z_grp[s][:])
+
+        def out_pass(s, m):
+            if s == 0:
+                out_acc[m] = psum.tile([P, S], F32, name="out_acc", tag="bank")
+            cols = slice(m * P, (m + 1) * P)
+            nc.tensor.matmul_mx(
+                out=out_acc[m][:, :V],
+                lhsT=w2_codes[s][:, cols].bitcast(FP8X4),
+                lhsT_scale=w2_scales[s][:, cols],
+                rhs=z_codes[s][:].bitcast(FP8X4),
+                rhs_scale=z_scales[s][:],
+                start=(s == 0),
+                stop=(s == PASSES - 1),
+            )
+
+        def side(b):
+            if b == 0:
+                group_w1(2, 0, 0, 256)
+                group_w1(2, 1, 0, 256)
+                quantize_w1(2)
+            elif b in (1, 2):
+                s = b - 1
+                group_w1(3, s, 0, 256)
+                group_w1(3, s, 256, 512)
+                if s == 1:
+                    quantize_w1(3)
+            elif b in (4, 5):
+                s = b - 4
+                group_w2(s, 0, 256)
+                group_w2(s, 256, 512)
+                quantize_w2(s)
+
+        h_next = project(0)
+        for s in range(PASSES):
+            group_w1(1, s, 0, W1_CHUNKS[1])
+        quantize_w1(1)
+        for b in range(BLOCKS):
+            if b % PACK == 0:
+                z_ps = [psum.tile([P, K_PASS], F32, name=f"z_ps{v}", tag=f"z_ps{v}", bufs=1) for v in range(HALVES)]
+            h = h_next
+            if b + 1 < BLOCKS:
+                h_next = project(b + 1)
+            gather_block(b, h)
+            side(b)
+            s = b // PACK
+            if b == PACK - 1:
+                for v in range(HALVES):
+                    z_out(s, v, 0, PACK)
+                z_finish(s)
+            if b == BLOCKS - 2:
+                for v in range(HALVES):
+                    z_out(s, v, 0, PACK - 1)
+                for m in range(N // P):
+                    out_pass(0, m)
+        for v in range(HALVES):
+            z_out(PASSES - 1, v, PACK - 1, PACK)
+        z_finish(PASSES - 1)
+        result = keep.tile([P, N // P, V], F32, name="result")
+        for m in range(N // P):
+            out_pass(1, m)
+            copy = (nc.scalar.copy, nc.vector.tensor_copy)[m % 2]
+            copy(out=result[:, m, :], in_=out_acc[m][:, :V])
+            nc.sync.dma_start(out=out[m * P : (m + 1) * P, :], in_=result[:, m, :])

@@ -20,7 +20,7 @@ FP8X4 = mybir.dt.float8_e4m3fn_x4
 RELU = mybir.ActivationFunctionType.Relu
 MULT = mybir.AluOpType.mult
 
-W1_CHUNKS = (128, 128, 256, 512)
+W1_LOADS = (1, 1, 1, 1, 4)
 
 
 def tile_picked_sage_relu_e_kernel(
@@ -45,62 +45,68 @@ def tile_picked_sage_relu_e_kernel(
         nc.scalar.activation(warm_out[:], warm[:], RELU)
 
         x_raw = [[keep.tile([P, T], F32, name=f"x_raw{s}_{j}") for j in range(PACK)] for s in range(PASSES)]
-        w1_raw = [keep.tile([P, PASSES, PACK, w], F32, name=f"w1_raw{c}") for c, w in enumerate(W1_CHUNKS)]
+        w1_raw = [keep.tile([P, PASSES, PACK, n * P], F32, name=f"w1_raw{c}") for c, n in enumerate(W1_LOADS)]
         w2_raw = [keep.tile([P, PACK, N], F32, name=f"w2_raw{s}") for s in range(PASSES)]
         gate_sb = keep.tile([P, D, V], F32, name="gate_sb")
+        home = [(c, i) for c, n in enumerate(W1_LOADS) for i in range(n)]
 
         def load_x(s, j):
             rows = xT[s * K_PASS : (s + 1) * K_PASS, :].rearrange("(p j) t -> j p t", j=PACK)
             nc.sync.dma_start(out=x_raw[s][j][:], in_=rows[j])
 
-        def load_w1(c, s_range=range(PASSES)):
-            first = sum(W1_CHUNKS[:c])
-            for s in s_range:
-                block = w1[s * K_PASS : (s + 1) * K_PASS, first : first + W1_CHUNKS[c]]
-                nc.sync.dma_start(out=w1_raw[c][:, s], in_=block.rearrange("(p j) m -> p j m", j=PACK))
+        def load_w1(c, s):
+            first = sum(W1_LOADS[:c]) * P
+            block = w1[s * K_PASS : (s + 1) * K_PASS, first : first + W1_LOADS[c] * P]
+            nc.sync.dma_start(out=w1_raw[c][:, s], in_=block.rearrange("(p j) m -> p j m", j=PACK))
 
         nc.sync.dma_start(offs_sb[:], offs)
         for s in range(PASSES):
             for j in range(PACK):
                 if (s, j) == (PASSES - 1, PACK - 1):
-                    load_w1(0, (0,))
+                    load_w1(0, 0)
                 load_x(s, j)
                 if (s, j) == (0, 0):
                     for d, pos in enumerate((pos1, pos2, pos3, pos4)):
                         nc.sync.dma_start(pos_sb[d][:], pos)
-        load_w1(0, (1,))
-        nc.sync.dma_start(out=gate_sb[:], in_=gate.rearrange("d p v -> p d v"))
-        for c in range(1, len(W1_CHUNKS)):
-            load_w1(c)
+        load_w1(0, 1)
+        for c in range(1, len(W1_LOADS)):
+            for s in range(PASSES):
+                load_w1(c, s)
+            if c == 1:
+                nc.sync.dma_start(out=gate_sb[:], in_=gate.rearrange("d p v -> p d v"))
         for s in range(PASSES):
             nc.sync.dma_start(
                 out=w2_raw[s][:], in_=w2[s * K_PASS : (s + 1) * K_PASS, :].rearrange("(p j) n -> p j n", j=PACK)
             )
 
-        w1_grp = [keep.tile([P, PASSES, w, PACK], BF16, name=f"w1_grp{c}", align_bytes=64) for c, w in enumerate(W1_CHUNKS)]
-        w1_codes = [keep.tile([P, PASSES, w], U32, name=f"w1_codes{c}", align_bytes=64) for c, w in enumerate(W1_CHUNKS)]
-        w1_scales = [keep.tile([P, PASSES, w], U8, name=f"w1_scales{c}", align_bytes=64) for c, w in enumerate(W1_CHUNKS)]
+        w1_grp = [
+            keep.tile([P, PASSES, P, PACK], BF16, name=f"w1_grp{b}", tag=f"turn{b}", align_bytes=64)
+            for b in range(BLOCKS)
+        ]
+        w1_codes = [keep.tile([P, PASSES, P], U32, name=f"w1_codes{b}", align_bytes=64) for b in range(BLOCKS)]
+        w1_scales = [keep.tile([P, PASSES, P], U8, name=f"w1_scales{b}", align_bytes=64) for b in range(BLOCKS)]
         w2_grp = [keep.tile([P, N, PACK], BF16, name=f"w2_grp{s}", align_bytes=64) for s in range(PASSES)]
         w2_codes = [keep.tile([P, N], U32, name=f"w2_codes{s}", align_bytes=64) for s in range(PASSES)]
         w2_scales = [keep.tile([P, N], U8, name=f"w2_scales{s}", align_bytes=64) for s in range(PASSES)]
 
-        def group_w1(c, s, m0, m1):
+        def group_w1(b, s):
+            c, i = home[b]
             nc.scalar.copy(
-                out=w1_grp[c][:, s, m0:m1, :], in_=w1_raw[c][:, s, :, m0:m1].rearrange("p j m -> p m j")
+                out=w1_grp[b][:, s], in_=w1_raw[c][:, s, :, i * P : (i + 1) * P].rearrange("p j m -> p m j")
             )
 
-        def quantize_w1(c):
+        def quantize_w1(b):
             nc.vector.quantize_mx(
-                out=w1_codes[c][:].rearrange("p s m -> p (s m)").bitcast(FP8X4),
-                scales=w1_scales[c][:].rearrange("p s m -> p (s m)"),
-                in_=w1_grp[c][:].rearrange("p s m j -> p (s m j)"),
+                out=w1_codes[b][:].rearrange("p s m -> p (s m)").bitcast(FP8X4),
+                scales=w1_scales[b][:].rearrange("p s m -> p (s m)"),
+                in_=w1_grp[b][:].rearrange("p s m j -> p (s m j)"),
             )
 
-        def quantize_w1_pass(c, s):
+        def quantize_w1_pass(b, s):
             nc.vector.quantize_mx(
-                out=w1_codes[c][:, s].bitcast(FP8X4),
-                scales=w1_scales[c][:, s],
-                in_=w1_grp[c][:, s].rearrange("p m j -> p (m j)"),
+                out=w1_codes[b][:, s].bitcast(FP8X4),
+                scales=w1_scales[b][:, s],
+                in_=w1_grp[b][:, s].rearrange("p m j -> p (m j)"),
             )
 
         def group_w2(s, n0, n1):
@@ -121,10 +127,9 @@ def tile_picked_sage_relu_e_kernel(
             last = s == PASSES - 1
             for j in range(PACK):
                 if last and j == PACK - 1:
-                    for u in range(PASSES):
-                        group_w1(0, u, 0, W1_CHUNKS[0])
-                        if u == 0:
-                            quantize_w1_pass(0, u)
+                    group_w1(0, 0)
+                    quantize_w1_pass(0, 0)
+                    group_w1(0, 1)
                     for t in (0, 1):
                         nc.vector.tensor_copy(
                             x_grp[s][:, t * HALF : (t + 1) * HALF, j],
@@ -141,11 +146,7 @@ def tile_picked_sage_relu_e_kernel(
                     in_=x_grp[s][:, cols, :].rearrange("p t j -> p (t j)"),
                 )
 
-        starts = [sum(W1_CHUNKS[:c]) for c in range(len(W1_CHUNKS))]
-
         def project(b):
-            c = max(i for i in range(len(W1_CHUNKS)) if starts[i] <= b * P)
-            cols = slice(b * P - starts[c], b * P - starts[c] + P)
             h = hpool.tile([P, S], F32, name="h")
             width = HALF if b == 0 else S
             for t in range(S // width):
@@ -154,8 +155,8 @@ def tile_picked_sage_relu_e_kernel(
                 for s in range(PASSES):
                     nc.tensor.matmul_mx(
                         out=acc[:, :width],
-                        lhsT=w1_codes[c][:, s, cols].bitcast(FP8X4),
-                        lhsT_scale=w1_scales[c][:, s, cols],
+                        lhsT=w1_codes[b][:, s].bitcast(FP8X4),
+                        lhsT_scale=w1_scales[b][:, s],
                         rhs=x_codes[s][:, nodes].bitcast(FP8X4),
                         rhs_scale=x_scales[s][:, nodes],
                         start=(s == 0),
@@ -174,98 +175,130 @@ def tile_picked_sage_relu_e_kernel(
         z_scales = [keep.tile([P, V], U8, name=f"z_scales{s}", align_bytes=64) for s in range(PASSES)]
         out_acc = {}
 
+        def add_transposed(b, d, v, prod):
+            nc.tensor.matmul(
+                z_ps[v][:, (b % PACK) * P : (b % PACK + 1) * P],
+                prod,
+                ident[:],
+                start=(d == 0),
+                stop=(d == D - 1),
+                is_transpose=True,
+            )
+
         def gather_block(b, h):
             for d in range(D):
-                prod = prods.tile([P, V], F32, name="prod")
+                if d == 1 and b + 1 < BLOCKS:
+                    prod = keep.tile([P, V], F32, name="prod_turn", tag=f"turn{b + 1}", align_bytes=64)
+                else:
+                    prod = prods.tile([P, V], F32, name="prod")
                 nc.vector.tensor_tensor(prod[:], h[:].indirect(pos_sb[d][:]), gate_sb[:, d, :], MULT)
                 for v in range(HALVES):
-                    nc.tensor.matmul(
-                        z_ps[v][:, (b % PACK) * P : (b % PACK + 1) * P],
-                        prod[:, v * P : (v + 1) * P],
-                        ident[:],
-                        start=(d == 0),
-                        stop=(d == D - 1),
-                        is_transpose=True,
-                    )
+                    add_transposed(b, d, v, prod[:, v * P : (v + 1) * P])
+
+        def gather_half(b, h, v):
+            for d in range(D):
+                prod = prods.tile([P, P], F32, name="prod")
+                nc.vector.tensor_tensor(
+                    prod[:],
+                    h[:].indirect(pos_sb[d][:, v * P // 16 : (v + 1) * P // 16]),
+                    gate_sb[:, d, v * P : (v + 1) * P],
+                    MULT,
+                )
+                add_transposed(b, d, v, prod[:])
 
         def z_out(s, v, b0, b1):
-            eng = nc.vector.tensor_copy if (b1 == PACK and s == PASSES - 1 and v == 1) else nc.scalar.copy
-            eng(out=z_t[v][:, s * K_PASS + b0 * P : s * K_PASS + b1 * P], in_=z_ps[v][:, b0 * P : b1 * P])
+            nc.scalar.copy(
+                out=z_t[v][:, s * K_PASS + b0 * P : s * K_PASS + b1 * P], in_=z_ps[v][:, b0 * P : b1 * P]
+            )
 
-        def z_finish(s):
-            words = psum.tile([P, HALVES, 2, P], F32, name="words", tag="words", bufs=2)
-            for v in range(HALVES):
-                zw = z_t[v][:].bitcast(F32)
-                for u in range(2):
-                    nc.tensor.transpose(
-                        words[:, v, u, :], zw[:, s * (K_PASS // 2) + u : (s + 1) * (K_PASS // 2) : 2], ident[:]
-                    )
-            for v, copy in enumerate((nc.scalar.copy, nc.vector.tensor_copy)):
-                copy(
-                    out=z_grp[s][:, v * P * PACK : (v + 1) * P * PACK].bitcast(F32).rearrange("p (n u) -> p n u", u=2),
-                    in_=words[:, v].rearrange("p u n -> p n u"),
+        def z_words(s, v):
+            words = psum.tile([P, 2, P], F32, name="words", tag="words", bufs=2)
+            zw = z_t[v][:].bitcast(F32)
+            for u in range(2):
+                nc.tensor.transpose(
+                    words[:, u, :], zw[:, s * (K_PASS // 2) + u : (s + 1) * (K_PASS // 2) : 2], ident[:]
                 )
-            nc.vector.quantize_mx(out=z_codes[s][:].bitcast(FP8X4), scales=z_scales[s][:], in_=z_grp[s][:])
+            nc.scalar.copy(
+                out=z_grp[s][:, v * K_PASS : (v + 1) * K_PASS].bitcast(F32).rearrange("p (n u) -> p n u", u=2),
+                in_=words[:].rearrange("p u n -> p n u"),
+            )
 
-        def out_pass(s, m):
-            if s == 0:
-                out_acc[m] = psum.tile([P, S], F32, name="out_acc", tag="bank")
+        def quantize_z(s, v0, v1):
+            nc.vector.quantize_mx(
+                out=z_codes[s][:, v0 * P : v1 * P].bitcast(FP8X4),
+                scales=z_scales[s][:, v0 * P : v1 * P],
+                in_=z_grp[s][:, v0 * K_PASS : v1 * K_PASS],
+            )
+
+        def out_pass(s, m, v):
             cols = slice(m * P, (m + 1) * P)
+            nodes = slice(v * P, (v + 1) * P)
             nc.tensor.matmul_mx(
-                out=out_acc[m][:, :V],
+                out=out_acc[m][:, nodes],
                 lhsT=w2_codes[s][:, cols].bitcast(FP8X4),
                 lhsT_scale=w2_scales[s][:, cols],
-                rhs=z_codes[s][:].bitcast(FP8X4),
-                rhs_scale=z_scales[s][:],
+                rhs=z_codes[s][:, nodes].bitcast(FP8X4),
+                rhs_scale=z_scales[s][:, nodes],
                 start=(s == 0),
                 stop=(s == PASSES - 1),
             )
 
-        def side(b):
-            if b == 0:
-                group_w1(2, 0, 0, 256)
-                group_w1(2, 1, 0, 256)
-                quantize_w1(2)
-            elif b in (1, 2):
-                s = b - 1
-                group_w1(3, s, 0, 256)
-                group_w1(3, s, 256, 512)
-                if s == 1:
-                    quantize_w1(3)
-            elif b in (4, 5):
-                s = b - 4
-                group_w2(s, 0, 256)
-                group_w2(s, 256, 512)
-                quantize_w2(s)
+        LAST = PASSES - 1
+        M_TILES = N // P
+        result = [keep.tile([P, M_TILES, P], F32, name=f"result{v}") for v in range(HALVES)]
+
+        def finish_half(v):
+            z_out(LAST, v, PACK - 1, PACK)
+            z_words(LAST, v)
+            quantize_z(LAST, v, v + 1)
+            for m in range(M_TILES):
+                out_pass(LAST, m, v)
+                copy = (nc.scalar.copy, nc.vector.tensor_copy)[m % 2]
+                copy(out=result[v][:, m, :], in_=out_acc[m][:, v * P : (v + 1) * P])
+                nc.sync.dma_start(out=out[m * P : (m + 1) * P, v * P : (v + 1) * P], in_=result[v][:, m, :])
+                if v + 1 < HALVES:
+                    out_pass(0, m, v + 1)
 
         h_next = project(0)
         for s in range(PASSES):
-            group_w1(1, s, 0, W1_CHUNKS[1])
+            group_w1(1, s)
         quantize_w1(1)
         for b in range(BLOCKS):
             if b % PACK == 0:
                 z_ps = [psum.tile([P, K_PASS], F32, name=f"z_ps{v}", tag=f"z_ps{v}", bufs=1) for v in range(HALVES)]
             h = h_next
+            if b + 2 < BLOCKS:
+                for s in range(PASSES):
+                    group_w1(b + 2, s)
             if b + 1 < BLOCKS:
                 h_next = project(b + 1)
-            gather_block(b, h)
-            side(b)
-            s = b // PACK
+            if b == BLOCKS - 1:
+                for v in range(HALVES):
+                    gather_half(b, h, v)
+                    if v == 0:
+                        finish_half(v)
+            else:
+                gather_block(b, h)
+            if b + 2 < BLOCKS:
+                quantize_w1(b + 2)
             if b == PACK - 1:
                 for v in range(HALVES):
-                    z_out(s, v, 0, PACK)
-                z_finish(s)
-            if b == BLOCKS - 2:
+                    z_out(0, v, 0, PACK)
+            if b == PACK:
                 for v in range(HALVES):
-                    z_out(s, v, 0, PACK - 1)
-                for m in range(N // P):
-                    out_pass(0, m)
-        for v in range(HALVES):
-            z_out(PASSES - 1, v, PACK - 1, PACK)
-        z_finish(PASSES - 1)
-        result = keep.tile([P, N // P, V], F32, name="result")
-        for m in range(N // P):
-            out_pass(1, m)
-            copy = (nc.scalar.copy, nc.vector.tensor_copy)[m % 2]
-            copy(out=result[:, m, :], in_=out_acc[m][:, :V])
-            nc.sync.dma_start(out=out[m * P : (m + 1) * P, :], in_=result[:, m, :])
+                    z_words(0, v)
+                quantize_z(0, 0, HALVES)
+            if b in (2, 4):
+                group_w2(0, (b // 2 - 1) * HALF, (b // 2) * HALF)
+            if b == 5:
+                quantize_w2(0)
+            if b == 6:
+                for n in (0, 1):
+                    group_w2(1, n * HALF, (n + 1) * HALF)
+                quantize_w2(1)
+                for v in range(HALVES):
+                    z_out(LAST, v, 0, PACK - 1)
+                for m in range(M_TILES):
+                    out_acc[m] = psum.tile([P, S], F32, name="out_acc", tag="bank")
+                    out_pass(0, m, 0)
+        finish_half(1)

@@ -9,6 +9,7 @@ PACK = 4
 K_PASS = P * PACK
 PASSES = K // K_PASS
 BLOCKS = H // P
+HALVES = V // P
 FLOPS = 2 * S * K * H + 2 * V * H * N + 2 * D * V * H
 
 F32 = mybir.dt.float32
@@ -20,7 +21,8 @@ FP8X4 = mybir.dt.float8_e4m3fn_x4
 RELU = mybir.ActivationFunctionType.Relu
 MULT = mybir.AluOpType.mult
 
-W1_LOADS = (1, 1, 1, 1, 4)
+W2_AFTER = (4, 5)
+W1_LOADS = (1, 1, 1, 1, 2, 2)
 
 
 def tile_picked_sage_relu_e_kernel(
@@ -47,6 +49,9 @@ def tile_picked_sage_relu_e_kernel(
         x_raw = [[keep.tile([P, T], F32, name=f"x_raw{s}_{j}") for j in range(PACK)] for s in range(PASSES)]
         w1_raw = [keep.tile([P, PASSES, PACK, n * P], F32, name=f"w1_raw{c}") for c, n in enumerate(W1_LOADS)]
         w2_raw = [keep.tile([P, PACK, N], F32, name=f"w2_raw{s}") for s in range(PASSES)]
+        gate_rows = keep.tile([P, P], F32, name="gate_rows")
+        nc.gpsimd.memset(gate_rows[:], 0.0)
+        gate_cols = keep.tile([P, D * HALVES], F32, name="gate_cols")
         gate_sb = keep.tile([P, D, V], F32, name="gate_sb")
         home = [(c, i) for c, n in enumerate(W1_LOADS) for i in range(n)]
 
@@ -62,18 +67,19 @@ def tile_picked_sage_relu_e_kernel(
         nc.sync.dma_start(offs_sb[:], offs)
         for s in range(PASSES):
             for j in range(PACK):
-                if (s, j) == (PASSES - 1, PACK - 1):
-                    load_w1(0, 0)
                 load_x(s, j)
-                if (s, j) == (0, 0):
+                if (s, j) == (0, 1):
+                    for d in range(D):
+                        nc.sync.dma_start(
+                            out=gate_rows[HALVES * d : HALVES * (d + 1), :],
+                            in_=gate[d, 0, :].rearrange("(v n) -> v n", v=HALVES),
+                        )
+                if (s, j) == (0, 3):
                     for d, pos in enumerate((pos1, pos2, pos3, pos4)):
                         nc.sync.dma_start(pos_sb[d][:], pos)
-        load_w1(0, 1)
-        for c in range(1, len(W1_LOADS)):
+        for c in range(len(W1_LOADS)):
             for s in range(PASSES):
                 load_w1(c, s)
-            if c == 1:
-                nc.sync.dma_start(out=gate_sb[:], in_=gate.rearrange("d p v -> p d v"))
         for s in range(PASSES):
             nc.sync.dma_start(
                 out=w2_raw[s][:], in_=w2[s * K_PASS : (s + 1) * K_PASS, :].rearrange("(p j) n -> p j n", j=PACK)
@@ -85,14 +91,15 @@ def tile_picked_sage_relu_e_kernel(
         ]
         w1_codes = [keep.tile([P, PASSES, P], U32, name=f"w1_codes{b}", align_bytes=64) for b in range(BLOCKS)]
         w1_scales = [keep.tile([P, PASSES, P], U8, name=f"w1_scales{b}", align_bytes=64) for b in range(BLOCKS)]
-        w2_grp = [keep.tile([P, N, PACK], BF16, name=f"w2_grp{s}", align_bytes=64) for s in range(PASSES)]
+        w2_grp = {}
         w2_codes = [keep.tile([P, N], U32, name=f"w2_codes{s}", align_bytes=64) for s in range(PASSES)]
         w2_scales = [keep.tile([P, N], U8, name=f"w2_scales{s}", align_bytes=64) for s in range(PASSES)]
 
         def group_w1(b, s):
             c, i = home[b]
             nc.scalar.copy(
-                out=w1_grp[b][:, s], in_=w1_raw[c][:, s, :, i * P : (i + 1) * P].rearrange("p j m -> p m j")
+                out=w1_grp[b][:, s].rearrange("p (c i) j -> p c j i", i=4),
+                in_=w1_raw[c][:, s, :, i * P : (i + 1) * P].rearrange("p j (c i) -> p c j i", i=4),
             )
 
         def quantize_w1(b):
@@ -110,7 +117,14 @@ def tile_picked_sage_relu_e_kernel(
             )
 
         def group_w2(s, n0, n1):
-            nc.scalar.copy(out=w2_grp[s][:, n0:n1, :], in_=w2_raw[s][:, :, n0:n1].rearrange("p j n -> p n j"))
+            if n0 == 0:
+                w2_grp[s] = keep.tile(
+                    [P, N, PACK], BF16, name=f"w2_grp{s}", tag=f"h_turn{W2_AFTER[s]}", align_bytes=64
+                )
+            nc.scalar.copy(
+                out=w2_grp[s][:, n0:n1, :].rearrange("p (c i) j -> p c j i", i=4),
+                in_=w2_raw[s][:, :, n0:n1].rearrange("p j (c i) -> p c j i", i=4),
+            )
 
         def quantize_w2(s):
             nc.vector.quantize_mx(
@@ -118,6 +132,16 @@ def tile_picked_sage_relu_e_kernel(
                 scales=w2_scales[s][:],
                 in_=w2_grp[s][:].rearrange("p n j -> p (n j)"),
             )
+
+        spread = psum.tile([P, P], F32, name="spread", tag="bank")
+        nc.tensor.transpose(spread[:], gate_rows[:], ident[:])
+        nc.scalar.copy(out=gate_cols[:], in_=spread[:, : D * HALVES])
+        for g in range(D // 2):
+            spread = psum.tile([P, 2 * V], F32, name="spread", tag="bank")
+            for r in range(2 * HALVES):
+                column = gate_cols[:, 2 * HALVES * g + r : 2 * HALVES * g + r + 1]
+                nc.tensor.transpose(spread[:, r * P : (r + 1) * P], column.to_broadcast([P, P]), ident[:])
+            nc.scalar.copy(out=gate_sb[:, 2 * g : 2 * g + 2, :].rearrange("p d v -> p (d v)"), in_=spread[:])
 
         x_grp = [keep.tile([P, S, PACK], BF16, name=f"x_grp{s}", align_bytes=64) for s in range(PASSES)]
         x_codes = [keep.tile([P, S], U32, name=f"x_codes{s}", align_bytes=64) for s in range(PASSES)]
@@ -147,7 +171,10 @@ def tile_picked_sage_relu_e_kernel(
                 )
 
         def project(b):
-            h = hpool.tile([P, S], F32, name="h")
+            if b in W2_AFTER:
+                h = keep.tile([P, S], F32, name="h_turn", tag=f"h_turn{b}", align_bytes=64)
+            else:
+                h = hpool.tile([P, S], F32, name="h")
             width = HALF if b == 0 else S
             for t in range(S // width):
                 acc = psum.tile([P, S], F32, name="acc", tag="bank")
@@ -162,13 +189,12 @@ def tile_picked_sage_relu_e_kernel(
                         start=(s == 0),
                         stop=(s == PASSES - 1),
                     )
-                if t == 0:
+                if b > 0:
                     nc.scalar.activation(h[:, nodes], acc[:, :width], RELU)
                 else:
                     nc.vector.tensor_relu(h[:, nodes], acc[:, :width])
             return h
 
-        HALVES = V // P
         z_t = [keep.tile([P, H], BF16, name=f"z_t{v}", align_bytes=64) for v in range(HALVES)]
         z_grp = [keep.tile([P, V * PACK], BF16, name=f"z_grp{s}", align_bytes=64) for s in range(PASSES)]
         z_codes = [keep.tile([P, V], U32, name=f"z_codes{s}", align_bytes=64) for s in range(PASSES)]
@@ -212,7 +238,10 @@ def tile_picked_sage_relu_e_kernel(
             )
 
         def z_words(s, v):
-            words = psum.tile([P, 2, P], F32, name="words", tag="words", bufs=2)
+            if s == LAST:
+                words = psum.tile([P, 2, P], F32, name="words", tag=f"z_ps{v}", bufs=2)
+            else:
+                words = psum.tile([P, 2, P], F32, name="words", tag="bank")
             zw = z_t[v][:].bitcast(F32)
             for u in range(2):
                 nc.tensor.transpose(
@@ -265,7 +294,7 @@ def tile_picked_sage_relu_e_kernel(
         quantize_w1(1)
         for b in range(BLOCKS):
             if b % PACK == 0:
-                z_ps = [psum.tile([P, K_PASS], F32, name=f"z_ps{v}", tag=f"z_ps{v}", bufs=1) for v in range(HALVES)]
+                z_ps = [psum.tile([P, K_PASS], F32, name=f"z_ps{v}", tag=f"z_ps{v}", bufs=2) for v in range(HALVES)]
             h = h_next
             if b + 2 < BLOCKS:
                 for s in range(PASSES):
@@ -288,14 +317,12 @@ def tile_picked_sage_relu_e_kernel(
                 for v in range(HALVES):
                     z_words(0, v)
                 quantize_z(0, 0, HALVES)
-            if b in (2, 4):
-                group_w2(0, (b // 2 - 1) * HALF, (b // 2) * HALF)
-            if b == 5:
-                quantize_w2(0)
-            if b == 6:
+            if b in W2_AFTER:
+                s = W2_AFTER.index(b)
                 for n in (0, 1):
-                    group_w2(1, n * HALF, (n + 1) * HALF)
-                quantize_w2(1)
+                    group_w2(s, n * HALF, (n + 1) * HALF)
+                quantize_w2(s)
+            if b == 6:
                 for v in range(HALVES):
                     z_out(LAST, v, 0, PACK - 1)
                 for m in range(M_TILES):

from contextlib import ExitStack

import concourse.mybir as mybir
from concourse.masks import make_identity

K, T, D, S, V, H, N = 1024, 2048, 4, 512, 256, 1024, 512
P = 128
PACK = 4
K_PASS = P * PACK
PASSES = K // K_PASS
BLOCKS = H // P
HALVES = V // P
FLOPS = 2 * S * K * H + 2 * V * H * N + 2 * D * V * H

F32 = mybir.dt.float32
BF16 = mybir.dt.bfloat16
U32 = mybir.dt.uint32
U16 = mybir.dt.uint16
U8 = mybir.dt.uint8
FP8X4 = mybir.dt.float8_e4m3fn_x4
RELU = mybir.ActivationFunctionType.Relu
MULT = mybir.AluOpType.mult

W2_AFTER = (4, 5)
W1_LOADS = (1, 1, 1, 1, 2, 2)


def tile_picked_sage_relu_e_kernel(
    tc, xT, w1, w2, gate, offs, pos1, pos2, pos3, pos4, out
):
    nc = tc.nc
    with ExitStack() as ctx:
        lists = ctx.enter_context(tc.tile_pool(name="lists", bufs=1))
        keep = ctx.enter_context(tc.tile_pool(name="keep", bufs=1))
        hpool = ctx.enter_context(tc.tile_pool(name="hpool", bufs=4))
        prods = ctx.enter_context(tc.tile_pool(name="prods", bufs=12))
        psum = ctx.enter_context(tc.psum_pool(name="psum", bufs=4))

        offs_sb = lists.tile([P, S // 16], U16, name="offs_sb")
        pos_sb = [lists.tile([P, V // 16], U16, name=f"pos_sb{d}") for d in range(D)]

        ident = keep.tile([P, P], F32, name="ident")
        make_identity(nc, ident[:])
        warm = keep.tile([P, 1], F32, name="warm")
        nc.gpsimd.memset(warm[:], 0.0)
        warm_out = keep.tile([P, 1], F32, name="warm_out")
        nc.scalar.activation(warm_out[:], warm[:], RELU)

        x_raw = [[keep.tile([P, T], F32, name=f"x_raw{s}_{j}") for j in range(PACK)] for s in range(PASSES)]
        w1_raw = [keep.tile([P, PASSES, PACK, n * P], F32, name=f"w1_raw{c}") for c, n in enumerate(W1_LOADS)]
        w2_raw = [keep.tile([P, PACK, N], F32, name=f"w2_raw{s}") for s in range(PASSES)]
        gate_rows = keep.tile([P, P], F32, name="gate_rows")
        nc.gpsimd.memset(gate_rows[:], 0.0)
        gate_cols = keep.tile([P, D * HALVES], F32, name="gate_cols")
        gate_sb = keep.tile([P, D, V], F32, name="gate_sb")
        home = [(c, i) for c, n in enumerate(W1_LOADS) for i in range(n)]

        def load_x(s, j):
            rows = xT[s * K_PASS : (s + 1) * K_PASS, :].rearrange("(p j) t -> j p t", j=PACK)
            nc.sync.dma_start(out=x_raw[s][j][:], in_=rows[j])

        def load_w1(c, s):
            first = sum(W1_LOADS[:c]) * P
            block = w1[s * K_PASS : (s + 1) * K_PASS, first : first + W1_LOADS[c] * P]
            nc.sync.dma_start(out=w1_raw[c][:, s], in_=block.rearrange("(p j) m -> p j m", j=PACK))

        nc.sync.dma_start(offs_sb[:], offs)
        for s in range(PASSES):
            for j in range(PACK):
                load_x(s, j)
                if (s, j) == (0, 1):
                    for d in range(D):
                        nc.sync.dma_start(
                            out=gate_rows[HALVES * d : HALVES * (d + 1), :],
                            in_=gate[d, 0, :].rearrange("(v n) -> v n", v=HALVES),
                        )
                if (s, j) == (0, 3):
                    for d, pos in enumerate((pos1, pos2, pos3, pos4)):
                        nc.sync.dma_start(pos_sb[d][:], pos)
        for c in range(len(W1_LOADS)):
            for s in range(PASSES):
                load_w1(c, s)
        for s in range(PASSES):
            nc.sync.dma_start(
                out=w2_raw[s][:], in_=w2[s * K_PASS : (s + 1) * K_PASS, :].rearrange("(p j) n -> p j n", j=PACK)
            )

        w1_grp = [
            keep.tile([P, PASSES, P, PACK], BF16, name=f"w1_grp{b}", tag=f"turn{b}", align_bytes=64)
            for b in range(BLOCKS)
        ]
        w1_codes = [keep.tile([P, PASSES, P], U32, name=f"w1_codes{b}", align_bytes=64) for b in range(BLOCKS)]
        w1_scales = [keep.tile([P, PASSES, P], U8, name=f"w1_scales{b}", align_bytes=64) for b in range(BLOCKS)]
        w2_grp = {}
        w2_codes = [keep.tile([P, N], U32, name=f"w2_codes{s}", align_bytes=64) for s in range(PASSES)]
        w2_scales = [keep.tile([P, N], U8, name=f"w2_scales{s}", align_bytes=64) for s in range(PASSES)]

        def group_w1(b, s):
            c, i = home[b]
            nc.scalar.copy(
                out=w1_grp[b][:, s].rearrange("p (c i) j -> p c j i", i=4),
                in_=w1_raw[c][:, s, :, i * P : (i + 1) * P].rearrange("p j (c i) -> p c j i", i=4),
            )

        def quantize_w1(b):
            nc.vector.quantize_mx(
                out=w1_codes[b][:].rearrange("p s m -> p (s m)").bitcast(FP8X4),
                scales=w1_scales[b][:].rearrange("p s m -> p (s m)"),
                in_=w1_grp[b][:].rearrange("p s m j -> p (s m j)"),
            )

        def quantize_w1_pass(b, s):
            nc.vector.quantize_mx(
                out=w1_codes[b][:, s].bitcast(FP8X4),
                scales=w1_scales[b][:, s],
                in_=w1_grp[b][:, s].rearrange("p m j -> p (m j)"),
            )

        def group_w2(s, n0, n1):
            if n0 == 0:
                w2_grp[s] = keep.tile(
                    [P, N, PACK], BF16, name=f"w2_grp{s}", tag=f"h_turn{W2_AFTER[s]}", align_bytes=64
                )
            nc.scalar.copy(
                out=w2_grp[s][:, n0:n1, :].rearrange("p (c i) j -> p c j i", i=4),
                in_=w2_raw[s][:, :, n0:n1].rearrange("p j (c i) -> p c j i", i=4),
            )

        def quantize_w2(s):
            nc.vector.quantize_mx(
                out=w2_codes[s][:].bitcast(FP8X4),
                scales=w2_scales[s][:],
                in_=w2_grp[s][:].rearrange("p n j -> p (n j)"),
            )

        spread = psum.tile([P, P], F32, name="spread", tag="bank")
        nc.tensor.transpose(spread[:], gate_rows[:], ident[:])
        nc.scalar.copy(out=gate_cols[:], in_=spread[:, : D * HALVES])
        for g in range(D // 2):
            spread = psum.tile([P, 2 * V], F32, name="spread", tag="bank")
            for r in range(2 * HALVES):
                column = gate_cols[:, 2 * HALVES * g + r : 2 * HALVES * g + r + 1]
                nc.tensor.transpose(spread[:, r * P : (r + 1) * P], column.to_broadcast([P, P]), ident[:])
            nc.scalar.copy(out=gate_sb[:, 2 * g : 2 * g + 2, :].rearrange("p d v -> p (d v)"), in_=spread[:])

        x_grp = [keep.tile([P, S, PACK], BF16, name=f"x_grp{s}", align_bytes=64) for s in range(PASSES)]
        x_codes = [keep.tile([P, S], U32, name=f"x_codes{s}", align_bytes=64) for s in range(PASSES)]
        x_scales = [keep.tile([P, S], U8, name=f"x_scales{s}", align_bytes=64) for s in range(PASSES)]
        HALF = S // 2
        for s in range(PASSES):
            last = s == PASSES - 1
            for j in range(PACK):
                if last and j == PACK - 1:
                    group_w1(0, 0)
                    quantize_w1_pass(0, 0)
                    group_w1(0, 1)
                    for t in (0, 1):
                        nc.vector.tensor_copy(
                            x_grp[s][:, t * HALF : (t + 1) * HALF, j],
                            x_raw[s][j][:].indirect(offs_sb[:, t * HALF // 16 : (t + 1) * HALF // 16]),
                        )
                    quantize_w1_pass(0, 1)
                else:
                    nc.vector.tensor_copy(x_grp[s][:, :, j], x_raw[s][j][:].indirect(offs_sb[:]))
            for t in (0, 1) if last else (None,):
                cols = slice(0, S) if t is None else slice(t * HALF, (t + 1) * HALF)
                nc.vector.quantize_mx(
                    out=x_codes[s][:, cols].bitcast(FP8X4),
                    scales=x_scales[s][:, cols],
                    in_=x_grp[s][:, cols, :].rearrange("p t j -> p (t j)"),
                )

        def project(b):
            if b in W2_AFTER:
                h = keep.tile([P, S], F32, name="h_turn", tag=f"h_turn{b}", align_bytes=64)
            else:
                h = hpool.tile([P, S], F32, name="h")
            width = HALF if b == 0 else S
            for t in range(S // width):
                acc = psum.tile([P, S], F32, name="acc", tag="bank")
                nodes = slice(t * width, (t + 1) * width)
                for s in range(PASSES):
                    nc.tensor.matmul_mx(
                        out=acc[:, :width],
                        lhsT=w1_codes[b][:, s].bitcast(FP8X4),
                        lhsT_scale=w1_scales[b][:, s],
                        rhs=x_codes[s][:, nodes].bitcast(FP8X4),
                        rhs_scale=x_scales[s][:, nodes],
                        start=(s == 0),
                        stop=(s == PASSES - 1),
                    )
                if b > 0:
                    nc.scalar.activation(h[:, nodes], acc[:, :width], RELU)
                else:
                    nc.vector.tensor_relu(h[:, nodes], acc[:, :width])
            return h

        z_t = [keep.tile([P, H], BF16, name=f"z_t{v}", align_bytes=64) for v in range(HALVES)]
        z_grp = [keep.tile([P, V * PACK], BF16, name=f"z_grp{s}", align_bytes=64) for s in range(PASSES)]
        z_codes = [keep.tile([P, V], U32, name=f"z_codes{s}", align_bytes=64) for s in range(PASSES)]
        z_scales = [keep.tile([P, V], U8, name=f"z_scales{s}", align_bytes=64) for s in range(PASSES)]
        out_acc = {}

        def add_transposed(b, d, v, prod):
            nc.tensor.matmul(
                z_ps[v][:, (b % PACK) * P : (b % PACK + 1) * P],
                prod,
                ident[:],
                start=(d == 0),
                stop=(d == D - 1),
                is_transpose=True,
            )

        def gather_block(b, h):
            for d in range(D):
                if d == 1 and b + 1 < BLOCKS:
                    prod = keep.tile([P, V], F32, name="prod_turn", tag=f"turn{b + 1}", align_bytes=64)
                else:
                    prod = prods.tile([P, V], F32, name="prod")
                nc.vector.tensor_tensor(prod[:], h[:].indirect(pos_sb[d][:]), gate_sb[:, d, :], MULT)
                for v in range(HALVES):
                    add_transposed(b, d, v, prod[:, v * P : (v + 1) * P])

        def gather_half(b, h, v):
            for d in range(D):
                prod = prods.tile([P, P], F32, name="prod")
                nc.vector.tensor_tensor(
                    prod[:],
                    h[:].indirect(pos_sb[d][:, v * P // 16 : (v + 1) * P // 16]),
                    gate_sb[:, d, v * P : (v + 1) * P],
                    MULT,
                )
                add_transposed(b, d, v, prod[:])

        def z_out(s, v, b0, b1):
            nc.scalar.copy(
                out=z_t[v][:, s * K_PASS + b0 * P : s * K_PASS + b1 * P], in_=z_ps[v][:, b0 * P : b1 * P]
            )

        def z_words(s, v):
            if s == LAST:
                words = psum.tile([P, 2, P], F32, name="words", tag=f"z_ps{v}", bufs=2)
            else:
                words = psum.tile([P, 2, P], F32, name="words", tag="bank")
            zw = z_t[v][:].bitcast(F32)
            for u in range(2):
                nc.tensor.transpose(
                    words[:, u, :], zw[:, s * (K_PASS // 2) + u : (s + 1) * (K_PASS // 2) : 2], ident[:]
                )
            nc.scalar.copy(
                out=z_grp[s][:, v * K_PASS : (v + 1) * K_PASS].bitcast(F32).rearrange("p (n u) -> p n u", u=2),
                in_=words[:].rearrange("p u n -> p n u"),
            )

        def quantize_z(s, v0, v1):
            nc.vector.quantize_mx(
                out=z_codes[s][:, v0 * P : v1 * P].bitcast(FP8X4),
                scales=z_scales[s][:, v0 * P : v1 * P],
                in_=z_grp[s][:, v0 * K_PASS : v1 * K_PASS],
            )

        def out_pass(s, m, v):
            cols = slice(m * P, (m + 1) * P)
            nodes = slice(v * P, (v + 1) * P)
            nc.tensor.matmul_mx(
                out=out_acc[m][:, nodes],
                lhsT=w2_codes[s][:, cols].bitcast(FP8X4),
                lhsT_scale=w2_scales[s][:, cols],
                rhs=z_codes[s][:, nodes].bitcast(FP8X4),
                rhs_scale=z_scales[s][:, nodes],
                start=(s == 0),
                stop=(s == PASSES - 1),
            )

        LAST = PASSES - 1
        M_TILES = N // P
        result = [keep.tile([P, M_TILES, P], F32, name=f"result{v}") for v in range(HALVES)]

        def finish_half(v):
            z_out(LAST, v, PACK - 1, PACK)
            z_words(LAST, v)
            quantize_z(LAST, v, v + 1)
            for m in range(M_TILES):
                out_pass(LAST, m, v)
                copy = (nc.scalar.copy, nc.vector.tensor_copy)[m % 2]
                copy(out=result[v][:, m, :], in_=out_acc[m][:, v * P : (v + 1) * P])
                nc.sync.dma_start(out=out[m * P : (m + 1) * P, v * P : (v + 1) * P], in_=result[v][:, m, :])
                if v + 1 < HALVES:
                    out_pass(0, m, v + 1)

        h_next = project(0)
        for s in range(PASSES):
            group_w1(1, s)
        quantize_w1(1)
        for b in range(BLOCKS):
            if b % PACK == 0:
                z_ps = [psum.tile([P, K_PASS], F32, name=f"z_ps{v}", tag=f"z_ps{v}", bufs=2) for v in range(HALVES)]
            h = h_next
            if b + 2 < BLOCKS:
                for s in range(PASSES):
                    group_w1(b + 2, s)
            if b + 1 < BLOCKS:
                h_next = project(b + 1)
            if b == BLOCKS - 1:
                for v in range(HALVES):
                    gather_half(b, h, v)
                    if v == 0:
                        finish_half(v)
            else:
                gather_block(b, h)
            if b + 2 < BLOCKS:
                quantize_w1(b + 2)
            if b == PACK - 1:
                for v in range(HALVES):
                    z_out(0, v, 0, PACK)
            if b == PACK:
                for v in range(HALVES):
                    z_words(0, v)
                quantize_z(0, 0, HALVES)
            if b in W2_AFTER:
                s = W2_AFTER.index(b)
                for n in (0, 1):
                    group_w2(s, n * HALF, (n + 1) * HALF)
                quantize_w2(s)
            if b == 6:
                for v in range(HALVES):
                    z_out(LAST, v, 0, PACK - 1)
                for m in range(M_TILES):
                    out_acc[m] = psum.tile([P, S], F32, name="out_acc", tag="bank")
                    out_pass(0, m, 0)
        finish_half(1)
